import numpy as np
import ml_dtypes


def mxq(x, axis, fmt="e4m3"):
    dtype, down = {"e4m3": (ml_dtypes.float8_e4m3fn, 7), "e5m2": (ml_dtypes.float8_e5m2, 14)}[fmt]
    v = np.moveaxis(np.asarray(x, np.float32).astype(ml_dtypes.bfloat16).astype(np.float64), axis, -1)
    blocks = v.reshape(v.shape[:-1] + (-1, 32))
    amax = np.abs(blocks).max(-1, keepdims=True)
    byte = np.maximum(np.where(amax > 0, np.frexp(amax)[1] - 1 + 127, 0) - down, 1)
    scale = np.exp2(byte - 127.0)
    codes = (blocks / scale).astype(np.float32).astype(dtype).astype(np.float64)
    return np.moveaxis((codes * scale).reshape(v.shape), -1, axis)


WIDE = False


def mx_kscale(k):
    if not WIDE:
        return np.ones(k)
    levels = np.array([10, -10, 5, -5, 0])
    if k % 512:
        return np.exp2(np.random.permutation(np.resize(levels, k // 32))).repeat(32)
    a = np.empty((k // 512, 16))
    for p in range(k // 512):
        a[p, :8] = np.random.permutation(np.resize(levels, 8))
        for g in range(8):
            far = levels[np.abs(levels - a[p, g]) >= 10]
            a[p, g + 8] = far[np.random.randint(len(far))]
    return np.exp2(a.ravel()).repeat(32)


def f64(x):
    return np.asarray(x).astype(np.float64)


def striped(idx):
    return np.tile(np.asarray(idx).reshape(-1, 16).T, (8, 1)).astype(np.uint16)


def unstriped(offs):
    return offs[:16].T.reshape(-1).astype(np.int64)


E2M1 = np.array([0.0, 0.5, 1.0, 1.5, 2.0, 3.0, 4.0, 6.0, -0.0, -0.5, -1.0, -1.5, -2.0, -3.0, -4.0, -6.0])


def pack_weight(w, fmt):
    k, n = w.shape
    w = f64(np.asarray(w, np.float32).astype(ml_dtypes.bfloat16)).reshape(k // 32, 32, n)
    amax = np.abs(w).max(1)
    if fmt == "e4m3":
        byte = np.frexp(amax)[1] - 1 + 127 - 7
    else:
        mant, ex = np.frexp(amax / 6.0)
        byte = np.where(mant > 0.5, ex, ex - 1) + 127
    byte = np.clip(np.where(amax > 0, byte, 1), 1, 254)
    scaled = (w * np.exp2(127.0 - byte)[:, None, :]).reshape(k, n).astype(np.float32)
    by_word = np.ascontiguousarray(scaled.reshape(k // 512, 128, 4, n).transpose(0, 1, 3, 2))
    if fmt == "e4m3":
        words = by_word.astype(ml_dtypes.float8_e4m3fn).view(np.uint8)
    else:
        c = by_word.astype(ml_dtypes.float4_e2m1fn).view(np.uint8) & 0xF
        words = (c[..., 0::2] | (c[..., 1::2] << 4)).reshape(k // 512, 128, 2 * n)
    return np.ascontiguousarray(words), np.ascontiguousarray(byte.astype(np.uint8).reshape(k // 512, 16, n))


def unpack_weight(words, scales, fmt):
    g, _, n = scales.shape
    words = np.ascontiguousarray(words).reshape(g, 128, n, -1)
    if fmt == "e4m3":
        vals = words.view(ml_dtypes.float8_e4m3fn).astype(np.float64)
    else:
        nib = np.empty((g, 128, n, 4), np.uint8)
        nib[..., 0::2] = words & 0xF
        nib[..., 1::2] = words >> 4
        vals = E2M1[nib]
    vals = vals * np.repeat(np.exp2(scales.astype(np.float64) - 127.0), 8, axis=1)[..., None]
    return vals.transpose(0, 1, 3, 2).reshape(g * 512, n)


K, R, F, T, J, G = 512, 128, 512, 2048, 512, 32


def setup_inputs():
    n = np.random.standard_normal
    idx = np.random.permutation(T)[:J]
    fk = mx_kscale(K)
    ff = mx_kscale(F)
    fj = mx_kscale(J)
    tj = np.ones(T)
    tj[idx] = fj
    tabp = pack_weight(n((K, T)) / fk[:, None], "e2m1")
    return {
        "tab_words": tabp[0],
        "tab_scales": tabp[1],
        "w1": (n((K, R)) * 1 / np.sqrt(K) * fk[:, None]).astype(np.float32),
        "sharp": (np.random.uniform(0.3, 1.5, (R, 1))).astype(np.float32),
        "wo": (n((F, R)) * 1 / np.sqrt(F) * ff[:, None]).astype(np.float32),
        "dy": (n((F, J)) / ff[:, None]).astype(np.float32),
        "js": (np.random.uniform(0.5, 2.0, (1, J)) * fj).astype(np.float32),
        "xrows": (n((K, T)) / tj).astype(np.float32),
        "old": (n((K, R)) * 4.0).astype(np.float32),
        "offs": striped(idx),
    }


def reference(tab_words, tab_scales, w1, sharp, wo, dy, js, xrows, old, offs):
    idx = unstriped(offs)
    tabu = unpack_weight(tab_words, tab_scales, "e2m1")
    w1q = mxq(f64(w1), 0, "e4m3")
    tabidxg = tabu[:, idx]
    a = w1q.T @ tabidxg
    m1 = a.reshape(R, G, J // G).mean(axis=2)
    mr = np.repeat(m1, J // G, axis=1)
    ce = a - mr
    woq = mxq(f64(wo), 0, "e4m3")
    dyq = mxq(f64(dy), 0, "e4m3")
    c0 = woq.T @ dyq
    dce = c0 * a / np.square(np.square(ce) * f64(sharp) + 1.0) * (-1.0) * f64(sharp) * ce * 2.0
    dmr = dce * (-1.0)
    dm1 = dmr.reshape(R, G, J // G).sum(axis=2)
    e1 = dm1 / 16.0
    r1 = np.repeat(e1, J // G, axis=1)
    da = c0 / (np.square(ce) * f64(sharp) + 1.0) + dce + r1
    gs = da * f64(js)
    gt1 = gs.T
    xt = f64(xrows)[:, idx].T
    xtq = mxq(xt, 0, "e4m3")
    gt1q = mxq(gt1, 0, "e4m3")
    gw = xtq.T @ gt1q
    y = gw + f64(old)
    return y

@@ -1,0 +1,191 @@
+from contextlib import ExitStack
+
+import concourse.mybir as mybir
+from concourse.masks import make_identity
+
+K, R, F, T, J, G = 512, 128, 512, 2048, 512, 32
+FLOPS = 3 * 2 * 512 * 128 * 512
+
+F32 = mybir.dt.float32
+BF16 = mybir.dt.bfloat16
+I32 = mybir.dt.int32
+U32 = mybir.dt.uint32
+U16 = mybir.dt.uint16
+U8 = mybir.dt.uint8
+FP8X4 = mybir.dt.float8_e4m3fn_x4
+FP4X4 = mybir.dt.float4_e2m1fn_x4
+ALU = mybir.AluOpType
+ACT = mybir.ActivationFunctionType
+AX = mybir.AxisListType
+
+P = 128
+PACK = 4
+GROUP = J // G
+
+
+def tile_attend_ccontrastpool_w_kernel(tc, tab_words, tab_scales, w1, sharp, wo, dy, js, xrows, old, offs, out):
+    nc = tc.nc
+    with ExitStack() as ctx:
+        sb = ctx.enter_context(tc.tile_pool(name="sb", bufs=1))
+        ps = ctx.enter_context(tc.psum_pool(name="ps", bufs=1))
+
+        def tile(shape, dtype, name, tag=None):
+            return sb.tile(shape, dtype, name=name, tag=tag or name, align_bytes=64)
+
+        offsets = sb.tile([P, J // 16], U16, name="offsets")
+        scale_win = tile([P, T], U8, "scale_win")
+        word_win = tile([P, T], U16, "word_win")
+        nc.gpsimd.memset(scale_win[:].bitcast(I32), 0)
+        warm = tile([P, 1], F32, "warm")
+        warm_out = tile([P, 1], F32, "warm_out")
+        nc.vector.memset(warm[:], 1.0)
+        nc.scalar.activation(warm_out[:], warm[:], ACT.Abs_reciprocal_sqrt)
+        ident = tile([P, P], F32, "ident")
+        make_identity(nc, ident[:])
+
+        nc.sync.dma_start(offsets[:], offs)
+        s = tile([P, 1], F32, "s")
+        nc.gpsimd.dma_start(s[:], sharp)
+        rows = tab_scales[0].rearrange("(q c) t -> c q t", c=4)
+        for c in range(4):
+            nc.sync.dma_start(scale_win[c:P:32, :].bitcast(I32), rows[c].bitcast(I32))
+        nc.sync.dma_start(word_win[:].bitcast(I32), tab_words[0].bitcast(I32))
+        w1_raw = tile([P, PACK, R], F32, "w1_raw")
+        nc.sync.dma_start(w1_raw[:], w1.rearrange("(p t) r -> p t r", t=PACK))
+        wo_raw = tile([P, PACK, R], F32, "wo_raw")
+        nc.sync.dma_start(wo_raw[:], wo.rearrange("(p t) r -> p t r", t=PACK))
+        half = J // 2
+        dy_raw = [tile([P, PACK, half], F32, "dy_raw%d" % h) for h in range(2)]
+        dy_v = dy.rearrange("(p t) j -> p t j", t=PACK)
+        for h in range(2):
+            nc.sync.dma_start(dy_raw[h][:], dy_v[:, :, h * half:(h + 1) * half])
+        x_v = xrows.rearrange("(p t) c -> t p c", t=PACK)
+        x_win = [tile([P, T], F32, "x_win%d" % t) for t in range(PACK)]
+        js_col = tile([P, PACK], F32, "js_col")
+        old_sb = tile([P, PACK, R], F32, "old_sb")
+        nc.sync.dma_start(x_win[0][:], x_v[0])
+        nc.gpsimd.dma_start(js_col[:], js.rearrange("o (p t) -> (o p) t", t=PACK))
+        for t in range(1, PACK):
+            nc.sync.dma_start(x_win[t][:], x_v[t])
+        nc.sync.dma_start(old_sb[:], old.rearrange("(p t) r -> p t r", t=PACK))
+
+        def interleave(copy, dst, src):
+            copy(dst.rearrange("p (c i t) -> p c t i", i=4, t=PACK), src.rearrange("p t (c i) -> p c t i", i=4))
+
+        def quantize(src, width, name, tag=None):
+            codes = tile([P, width], U32, name + "_codes", tag)
+            scales = tile([P, width], U8, name + "_scales")
+            nc.vector.quantize_mx(out=codes[:].bitcast(FP8X4), scales=scales[:], in_=src)
+            return codes, scales
+
+        tab_sc = tile([P, J], U8, "tab_sc")
+        tab_w = tile([P, J], U16, "tab_w")
+        nc.vector.tensor_copy(tab_sc[:], scale_win[:].indirect(offsets[:]))
+        nc.vector.tensor_copy(tab_w[:], word_win[:].indirect(offsets[:]))
+        w1_bf = tile([P, R * PACK], BF16, "w1_bf")
+        interleave(nc.scalar.copy, w1_bf[:], w1_raw[:])
+        w1_c, w1_s = quantize(w1_bf[:], R, "w1")
+        a_ps = ps.tile([P, J], F32, name="a_ps")
+        nc.tensor.matmul_mx(out=a_ps[:], lhsT=w1_c[:].bitcast(FP8X4), lhsT_scale=w1_s[:],
+                            rhs=tab_w[:].bitcast(FP4X4), rhs_scale=tab_sc[:], start=True, stop=True)
+        wo_bf = tile([P, R * PACK], BF16, "wo_bf")
+        interleave(nc.scalar.copy, wo_bf[:], wo_raw[:])
+        wo_c, wo_s = quantize(wo_bf[:], R, "wo")
+        dy_bf = tile([P, J * PACK], BF16, "dy_bf")
+        interleave(nc.scalar.copy, dy_bf[:, :half * PACK], dy_raw[0][:])
+        interleave(nc.scalar.copy, dy_bf[:, half * PACK:], dy_raw[1][:])
+
+        def dealt(ap):
+            return ap.rearrange("r (p t) -> r t p", t=PACK)
+
+        def planes(t_):
+            return t_[:].rearrange("r (t p) -> r t p", t=PACK)
+
+        a_sum = tile([P, G], F32, "a_sum")
+        nc.vector.tensor_reduce(a_sum[:], a_ps[:].rearrange("r (g i) -> r g i", i=GROUP), AX.X, ALU.add)
+        ce = tile([P, J], F32, "ce")
+        for t in range(PACK):
+            nc.vector.scalar_tensor_tensor(
+                planes(ce)[:, t, :].rearrange("r (g q) -> r g q", q=4), a_sum[:].unsqueeze(2).to_broadcast([P, G, 4]),
+                -1.0 / GROUP, dealt(a_ps[:])[:, t, :].rearrange("r (g q) -> r g q", q=4), ALU.mult, ALU.add)
+        sq = tile([P, J], F32, "sq")
+        den2 = tile([P, J], F32, "den2")
+        inv_abs = tile([P, J], F32, "inv_abs")
+        inv2 = tile([P, J], F32, "inv2")
+        halves = [slice(0, half), slice(half, J)]
+        for h in halves:
+            nc.scalar.activation(sq[:, h], ce[:, h], ACT.Square)
+        for h in halves:
+            nc.scalar.activation(den2[:, h], sq[:, h], ACT.Square, bias=1.0, scale=s[:])
+        for h in halves:
+            nc.scalar.activation(inv_abs[:, h], den2[:, h], ACT.Abs_reciprocal_sqrt)
+        for h in halves:
+            nc.scalar.activation(inv2[:, h], inv_abs[:, h], ACT.Square)
+        sca = tile([P, J], F32, "sca")
+        nc.vector.scalar_tensor_tensor(planes(sca), planes(ce), s[:], dealt(a_ps[:]), ALU.mult, ALU.mult)
+
+        dy_c, dy_s = quantize(dy_bf[:], J, "dy", "a_sum")
+        c_ps = ps.tile([P, J], F32, name="c_ps")
+        nc.tensor.matmul_mx(out=c_ps[:], lhsT=wo_c[:].bitcast(FP8X4), lhsT_scale=wo_s[:],
+                            rhs=dy_c[:].bitcast(FP8X4), rhs_scale=dy_s[:], start=True, stop=True)
+
+        after = {0: "dy_bf", 1: "x_win0", 2: "dce", 3: "x_win2"}
+        xt_bf = {}
+        x_g = {}
+
+        def bring_x(t):
+            x_g[t] = tile([P, J], BF16, "x_g%d" % t, after[t])
+            nc.vector.tensor_copy(x_g[t][:], x_win[t][:].indirect(offsets[:]))
+            pairs = x_g[t][:].bitcast(F32)
+            xt_bf[t] = tile([P, P * PACK], BF16, "xt_bf%d" % t, "inv_abs" if t == 0 else None)
+            xt_ps = ps.tile([P, 2, P], F32, name="xt_ps%d" % (t % 2))
+            for u in range(2):
+                nc.tensor.transpose(xt_ps[:, u, :], pairs[:, u::2], ident[:])
+            nc.scalar.copy(xt_bf[t][:].bitcast(F32).rearrange("p (k u) -> p k u", u=2), xt_ps[:].rearrange("p u k -> p k u"))
+
+        bring_x(0)
+        bring_x(1)
+
+        cv = tile([P, J], F32, "cv", "x_win1")
+        dce = tile([P, J], F32, "dce")
+        rest = tile([P, J], F32, "rest")
+        for n in range(2):
+            nc.vector.tensor_tensor(planes(cv)[:, 2 * n:2 * n + 2, :], dealt(c_ps[:])[:, 2 * n:2 * n + 2, :],
+                                    planes(inv2)[:, 2 * n:2 * n + 2, :], ALU.mult)
+        for h in halves:
+            nc.vector.scalar_tensor_tensor(dce[:, h], cv[:, h], -2.0, sca[:, h], ALU.mult, ALU.mult)
+        nc.vector.scalar_tensor_tensor(rest[:], sq[:], s[:], cv[:], ALU.mult, ALU.mult)
+        d_sum = tile([P, G], F32, "d_sum")
+        nc.vector.tensor_reduce(d_sum[:], dce[:].rearrange("r (t g q) -> r g t q", t=PACK, q=4), AX.XY, ALU.add)
+        back = tile([P, P], F32, "back")
+        nc.scalar.activation(back[:].rearrange("r (g q) -> r g q", q=4),
+                             d_sum[:].unsqueeze(2).to_broadcast([P, G, 4]), ACT.Copy, scale=-1.0 / GROUP)
+        da_ps = ps.tile([P, PACK, R], F32, name="da_ps")
+        terms = [cv, dce, rest]
+        for n, term in enumerate(terms):
+            for t in range(PACK):
+                nc.tensor.matmul(da_ps[:, t, :], term[:, t * P:(t + 1) * P], ident[:],
+                                 start=(n == 0 and t == 0), stop=False, is_transpose=True)
+        for t in range(PACK):
+            nc.tensor.matmul(da_ps[:, t, :], back[:], ident[:], start=False, stop=(t == PACK - 1), is_transpose=True)
+
+        xq = {t: quantize(xt_bf[t][:], P, "x%d" % t) for t in range(2)}
+        bring_x(2)
+        bring_x(3)
+        gt_bf = tile([P, R * PACK], BF16, "gt_bf", "x_win3")
+        nc.vector.tensor_tensor(gt_bf[:].rearrange("p (r t) -> p r t", t=PACK), da_ps[:].rearrange("p t r -> p r t"),
+                                js_col[:].unsqueeze(1).to_broadcast([P, R, PACK]), ALU.mult)
+        xq[2] = quantize(xt_bf[2][:], P, "x2", "js_col")
+        gt_c, gt_s = quantize(gt_bf[:], R, "gt")
+        xq[3] = quantize(xt_bf[3][:], P, "x3")
+
+        out_v = out.rearrange("(p t) r -> p t r", t=PACK)
+        for name, ts in (("early", slice(0, PACK - 1)), ("last", slice(PACK - 1, PACK))):
+            count = ts.stop - ts.start
+            gw_ps = ps.tile([P, count, R], F32, name="gw_ps_" + name)
+            for t in range(ts.start, ts.stop):
+                nc.tensor.matmul_mx(out=gw_ps[:, t - ts.start, :], lhsT=xq[t][0][:].bitcast(FP8X4), lhsT_scale=xq[t][1][:],
+                                    rhs=gt_c[:].bitcast(FP8X4), rhs_scale=gt_s[:], start=True, stop=True)
+            res = tile([P, count, R], F32, "res_" + name)
+            nc.vector.tensor_tensor(res[:], gw_ps[:], old_sb[:, ts, :], ALU.add)
+            nc.sync.dma_start(out_v[:, ts, :], res[:])

@@ -45,7 +45,6 @@ def tile_attend_ccontrastpool_w_kernel(tc, tab_words, tab_scales, w1, sharp, wo,
 
         nc.sync.dma_start(offsets[:], offs)
         s = tile([P, 1], F32, "s")
-        nc.gpsimd.dma_start(s[:], sharp)
         rows = tab_scales[0].rearrange("(q c) t -> c q t", c=4)
         for c in range(4):
             nc.sync.dma_start(scale_win[c:P:32, :].bitcast(I32), rows[c].bitcast(I32))
@@ -63,10 +62,11 @@ def tile_attend_ccontrastpool_w_kernel(tc, tab_words, tab_scales, w1, sharp, wo,
         x_win = [tile([P, T], F32, "x_win%d" % t) for t in range(PACK)]
         js_col = tile([P, PACK], F32, "js_col")
         old_sb = tile([P, PACK, R], F32, "old_sb")
-        nc.sync.dma_start(x_win[0][:], x_v[0])
-        nc.gpsimd.dma_start(js_col[:], js.rearrange("o (p t) -> (o p) t", t=PACK))
-        for t in range(1, PACK):
+        nc.sync.dma_start(s[:], sharp)
+        for t in range(PACK):
             nc.sync.dma_start(x_win[t][:], x_v[t])
+            if t == 1:
+                nc.sync.dma_start(js_col[:], js.rearrange("o (p t) -> (o p) t", t=PACK))
         nc.sync.dma_start(old_sb[:], old.rearrange("(p t) r -> p t r", t=PACK))
 
         def interleave(copy, dst, src):
@@ -91,8 +91,8 @@ def tile_attend_ccontrastpool_w_kernel(tc, tab_words, tab_scales, w1, sharp, wo,
         wo_bf = tile([P, R * PACK], BF16, "wo_bf")
         interleave(nc.scalar.copy, wo_bf[:], wo_raw[:])
         wo_c, wo_s = quantize(wo_bf[:], R, "wo")
-        dy_bf = tile([P, J * PACK], BF16, "dy_bf")
-        interleave(nc.scalar.copy, dy_bf[:, :half * PACK], dy_raw[0][:])
+        dy_bf = tile([P, J * PACK], BF16, "dy_bf", "w1_bf")
+        interleave(nc.vector.tensor_copy, dy_bf[:, :half * PACK], dy_raw[0][:])
         interleave(nc.scalar.copy, dy_bf[:, half * PACK:], dy_raw[1][:])
 
         def dealt(ap):
@@ -101,14 +101,14 @@ def tile_attend_ccontrastpool_w_kernel(tc, tab_words, tab_scales, w1, sharp, wo,
         def planes(t_):
             return t_[:].rearrange("r (t p) -> r t p", t=PACK)
 
-        a_sum = tile([P, G], F32, "a_sum")
+        a_sum = tile([P, G], F32, "a_sum", "dy_raw0")
         nc.vector.tensor_reduce(a_sum[:], a_ps[:].rearrange("r (g i) -> r g i", i=GROUP), AX.X, ALU.add)
         ce = tile([P, J], F32, "ce")
         for t in range(PACK):
             nc.vector.scalar_tensor_tensor(
                 planes(ce)[:, t, :].rearrange("r (g q) -> r g q", q=4), a_sum[:].unsqueeze(2).to_broadcast([P, G, 4]),
                 -1.0 / GROUP, dealt(a_ps[:])[:, t, :].rearrange("r (g q) -> r g q", q=4), ALU.mult, ALU.add)
-        sq = tile([P, J], F32, "sq")
+        sq = tile([P, J], F32, "sq", "dy_raw1")
         den2 = tile([P, J], F32, "den2")
         inv_abs = tile([P, J], F32, "inv_abs")
         inv2 = tile([P, J], F32, "inv2")
@@ -124,29 +124,34 @@ def tile_attend_ccontrastpool_w_kernel(tc, tab_words, tab_scales, w1, sharp, wo,
         sca = tile([P, J], F32, "sca")
         nc.vector.scalar_tensor_tensor(planes(sca), planes(ce), s[:], dealt(a_ps[:]), ALU.mult, ALU.mult)
 
-        dy_c, dy_s = quantize(dy_bf[:], J, "dy", "a_sum")
+        dy_c, dy_s = quantize(dy_bf[:], J, "dy", "dy_raw0")
         c_ps = ps.tile([P, J], F32, name="c_ps")
         nc.tensor.matmul_mx(out=c_ps[:], lhsT=wo_c[:].bitcast(FP8X4), lhsT_scale=wo_s[:],
                             rhs=dy_c[:].bitcast(FP8X4), rhs_scale=dy_s[:], start=True, stop=True)
 
-        after = {0: "dy_bf", 1: "x_win0", 2: "dce", 3: "x_win2"}
-        xt_bf = {}
         x_g = {}
 
-        def bring_x(t):
-            x_g[t] = tile([P, J], BF16, "x_g%d" % t, after[t])
+        def gather_x(t, tag):
+            x_g[t] = tile([P, J], BF16, "x_g%d" % t, tag)
             nc.vector.tensor_copy(x_g[t][:], x_win[t][:].indirect(offsets[:]))
-            pairs = x_g[t][:].bitcast(F32)
-            xt_bf[t] = tile([P, P * PACK], BF16, "xt_bf%d" % t, "inv_abs" if t == 0 else None)
-            xt_ps = ps.tile([P, 2, P], F32, name="xt_ps%d" % (t % 2))
-            for u in range(2):
-                nc.tensor.transpose(xt_ps[:, u, :], pairs[:, u::2], ident[:])
-            nc.scalar.copy(xt_bf[t][:].bitcast(F32).rearrange("p (k u) -> p k u", u=2), xt_ps[:].rearrange("p u k -> p k u"))
 
-        bring_x(0)
-        bring_x(1)
+        def turn_x(ts, dst):
+            name = "".join(str(t) for t in ts)
+            xt_ps = ps.tile([P, len(ts), 2, P], F32, name="xt_ps" + name)
+            for n, t in enumerate(ts):
+                pairs = x_g[t][:].bitcast(F32)
+                for u in range(2):
+                    nc.tensor.transpose(xt_ps[:, n, u, :], pairs[:, u::2], ident[:])
+            nc.scalar.copy(dst.bitcast(F32).rearrange("p (n k u) -> p n k u", k=P, u=2),
+                           xt_ps[:].rearrange("p n u k -> p n k u"))
 
-        cv = tile([P, J], F32, "cv", "x_win1")
+        gather_x(0, "w1_bf")
+        x1_bf = tile([P, T], BF16, "x1_bf", "inv_abs")
+        nc.scalar.copy(x1_bf[:], x_win[1][:])
+        x_g[1] = tile([P, J], BF16, "x_g1")
+        nc.scalar.activation(x_g[1][:], x1_bf[:].indirect(offsets[:]), ACT.Copy)
+
+        cv = tile([P, J], F32, "cv", "x_win0")
         dce = tile([P, J], F32, "dce")
         rest = tile([P, J], F32, "rest")
         for n in range(2):
@@ -154,12 +159,13 @@ def tile_attend_ccontrastpool_w_kernel(tc, tab_words, tab_scales, w1, sharp, wo,
                                     planes(inv2)[:, 2 * n:2 * n + 2, :], ALU.mult)
         for h in halves:
             nc.vector.scalar_tensor_tensor(dce[:, h], cv[:, h], -2.0, sca[:, h], ALU.mult, ALU.mult)
-        nc.vector.scalar_tensor_tensor(rest[:], sq[:], s[:], cv[:], ALU.mult, ALU.mult)
+        nc.vector.scalar_tensor_tensor(rest[:, halves[0]], sq[:, halves[0]], s[:], cv[:, halves[0]], ALU.mult, ALU.mult)
         d_sum = tile([P, G], F32, "d_sum")
         nc.vector.tensor_reduce(d_sum[:], dce[:].rearrange("r (t g q) -> r g t q", t=PACK, q=4), AX.XY, ALU.add)
+        nc.vector.scalar_tensor_tensor(rest[:, halves[1]], sq[:, halves[1]], s[:], cv[:, halves[1]], ALU.mult, ALU.mult)
         back = tile([P, P], F32, "back")
-        nc.scalar.activation(back[:].rearrange("r (g q) -> r g q", q=4),
-                             d_sum[:].unsqueeze(2).to_broadcast([P, G, 4]), ACT.Copy, scale=-1.0 / GROUP)
+        nc.vector.tensor_scalar(back[:].rearrange("r (g q) -> r g q", q=4),
+                                d_sum[:].unsqueeze(2).to_broadcast([P, G, 4]), -1.0 / GROUP, None, ALU.mult)
         da_ps = ps.tile([P, PACK, R], F32, name="da_ps")
         terms = [cv, dce, rest]
         for n, term in enumerate(terms):
@@ -169,23 +175,29 @@ def tile_attend_ccontrastpool_w_kernel(tc, tab_words, tab_scales, w1, sharp, wo,
         for t in range(PACK):
             nc.tensor.matmul(da_ps[:, t, :], back[:], ident[:], start=False, stop=(t == PACK - 1), is_transpose=True)
 
-        xq = {t: quantize(xt_bf[t][:], P, "x%d" % t) for t in range(2)}
-        bring_x(2)
-        bring_x(3)
-        gt_bf = tile([P, R * PACK], BF16, "gt_bf", "x_win3")
-        nc.vector.tensor_tensor(gt_bf[:].rearrange("p (r t) -> p r t", t=PACK), da_ps[:].rearrange("p t r -> p r t"),
+        gather_x(2, "sca")
+        x0_gt = tile([P, 2, P * PACK], BF16, "x0_gt", "x_win2")
+        turn_x([0], x0_gt[:, 0, :])
+        xt_21 = tile([P, 2 * P * PACK], BF16, "xt_21")
+        turn_x([2, 1], xt_21[:])
+        nc.vector.tensor_tensor(x0_gt[:, 1, :].rearrange("p (r t) -> p r t", t=PACK), da_ps[:].rearrange("p t r -> p r t"),
                                 js_col[:].unsqueeze(1).to_broadcast([P, R, PACK]), ALU.mult)
-        xq[2] = quantize(xt_bf[2][:], P, "x2", "js_col")
-        gt_c, gt_s = quantize(gt_bf[:], R, "gt")
-        xq[3] = quantize(xt_bf[3][:], P, "x3")
+        gather_x(3, None)
+        xt_3 = tile([P, P * PACK], BF16, "xt_3")
+        turn_x([3], xt_3[:])
+        c0g, s0g = quantize(x0_gt[:].rearrange("p n c -> p (n c)"), 2 * P, "x0gt", "x_win3")
+        gt_c, gt_s = c0g[:, P:], s0g[:, P:]
+        c21, s21 = quantize(xt_21[:], 2 * P, "x21", "x_win2")
+        c3, s3 = quantize(xt_3[:], P, "x3")
+        xq = {0: (c0g[:, :P], s0g[:, :P]), 1: (c21[:, P:], s21[:, P:]), 2: (c21[:, :P], s21[:, :P]), 3: (c3[:], s3[:])}
 
         out_v = out.rearrange("(p t) r -> p t r", t=PACK)
         for name, ts in (("early", slice(0, PACK - 1)), ("last", slice(PACK - 1, PACK))):
             count = ts.stop - ts.start
             gw_ps = ps.tile([P, count, R], F32, name="gw_ps_" + name)
             for t in range(ts.start, ts.stop):
-                nc.tensor.matmul_mx(out=gw_ps[:, t - ts.start, :], lhsT=xq[t][0][:].bitcast(FP8X4), lhsT_scale=xq[t][1][:],
-                                    rhs=gt_c[:].bitcast(FP8X4), rhs_scale=gt_s[:], start=True, stop=True)
+                nc.tensor.matmul_mx(out=gw_ps[:, t - ts.start, :], lhsT=xq[t][0].bitcast(FP8X4), lhsT_scale=xq[t][1],
+                                    rhs=gt_c.bitcast(FP8X4), rhs_scale=gt_s, start=True, stop=True)
             res = tile([P, count, R], F32, "res_" + name)
             nc.vector.tensor_tensor(res[:], gw_ps[:], old_sb[:, ts, :], ALU.add)
             nc.sync.dma_start(out_v[:, ts, :], res[:])

from contextlib import ExitStack

import concourse.mybir as mybir
from concourse.masks import make_identity

K, R, F, T, J, G = 512, 128, 512, 2048, 512, 32
FLOPS = 3 * 2 * 512 * 128 * 512

F32 = mybir.dt.float32
BF16 = mybir.dt.bfloat16
I32 = mybir.dt.int32
U32 = mybir.dt.uint32
U16 = mybir.dt.uint16
U8 = mybir.dt.uint8
FP8X4 = mybir.dt.float8_e4m3fn_x4
FP4X4 = mybir.dt.float4_e2m1fn_x4
ALU = mybir.AluOpType
ACT = mybir.ActivationFunctionType
AX = mybir.AxisListType

P = 128
PACK = 4
GROUP = J // G


def tile_attend_ccontrastpool_w_kernel(tc, tab_words, tab_scales, w1, sharp, wo, dy, js, xrows, old, offs, out):
    nc = tc.nc
    with ExitStack() as ctx:
        sb = ctx.enter_context(tc.tile_pool(name="sb", bufs=1))
        ps = ctx.enter_context(tc.psum_pool(name="ps", bufs=1))

        def tile(shape, dtype, name, tag=None):
            return sb.tile(shape, dtype, name=name, tag=tag or name, align_bytes=64)

        offsets = sb.tile([P, J // 16], U16, name="offsets")
        scale_win = tile([P, T], U8, "scale_win")
        word_win = tile([P, T], U16, "word_win")
        nc.gpsimd.memset(scale_win[:].bitcast(I32), 0)
        warm = tile([P, 1], F32, "warm")
        warm_out = tile([P, 1], F32, "warm_out")
        nc.vector.memset(warm[:], 1.0)
        nc.scalar.activation(warm_out[:], warm[:], ACT.Abs_reciprocal_sqrt)
        ident = tile([P, P], F32, "ident")
        make_identity(nc, ident[:])

        nc.sync.dma_start(offsets[:], offs)
        s = tile([P, 1], F32, "s")
        rows = tab_scales[0].rearrange("(q c) t -> c q t", c=4)
        for c in range(4):
            nc.sync.dma_start(scale_win[c:P:32, :].bitcast(I32), rows[c].bitcast(I32))
        nc.sync.dma_start(word_win[:].bitcast(I32), tab_words[0].bitcast(I32))
        w1_raw = tile([P, PACK, R], F32, "w1_raw")
        nc.sync.dma_start(w1_raw[:], w1.rearrange("(p t) r -> p t r", t=PACK))
        wo_raw = tile([P, PACK, R], F32, "wo_raw")
        nc.sync.dma_start(wo_raw[:], wo.rearrange("(p t) r -> p t r", t=PACK))
        half = J // 2
        dy_raw = [tile([P, PACK, half], F32, "dy_raw%d" % h) for h in range(2)]
        dy_v = dy.rearrange("(p t) j -> p t j", t=PACK)
        for h in range(2):
            nc.sync.dma_start(dy_raw[h][:], dy_v[:, :, h * half:(h + 1) * half])
        x_v = xrows.rearrange("(p t) c -> t p c", t=PACK)
        x_win = [tile([P, T], F32, "x_win%d" % t) for t in range(PACK)]
        js_col = tile([P, PACK], F32, "js_col")
        old_sb = tile([P, PACK, R], F32, "old_sb")
        nc.sync.dma_start(s[:], sharp)
        for t in range(PACK):
            nc.sync.dma_start(x_win[t][:], x_v[t])
            if t == 1:
                nc.sync.dma_start(js_col[:], js.rearrange("o (p t) -> (o p) t", t=PACK))
        nc.sync.dma_start(old_sb[:], old.rearrange("(p t) r -> p t r", t=PACK))

        def interleave(copy, dst, src):
            copy(dst.rearrange("p (c i t) -> p c t i", i=4, t=PACK), src.rearrange("p t (c i) -> p c t i", i=4))

        def quantize(src, width, name, tag=None):
            codes = tile([P, width], U32, name + "_codes", tag)
            scales = tile([P, width], U8, name + "_scales")
            nc.vector.quantize_mx(out=codes[:].bitcast(FP8X4), scales=scales[:], in_=src)
            return codes, scales

        tab_sc = tile([P, J], U8, "tab_sc")
        tab_w = tile([P, J], U16, "tab_w")
        nc.vector.tensor_copy(tab_sc[:], scale_win[:].indirect(offsets[:]))
        nc.vector.tensor_copy(tab_w[:], word_win[:].indirect(offsets[:]))
        w1_bf = tile([P, R * PACK], BF16, "w1_bf")
        interleave(nc.scalar.copy, w1_bf[:], w1_raw[:])
        w1_c, w1_s = quantize(w1_bf[:], R, "w1")
        a_ps = ps.tile([P, J], F32, name="a_ps")
        nc.tensor.matmul_mx(out=a_ps[:], lhsT=w1_c[:].bitcast(FP8X4), lhsT_scale=w1_s[:],
                            rhs=tab_w[:].bitcast(FP4X4), rhs_scale=tab_sc[:], start=True, stop=True)
        wo_bf = tile([P, R * PACK], BF16, "wo_bf")
        interleave(nc.scalar.copy, wo_bf[:], wo_raw[:])
        wo_c, wo_s = quantize(wo_bf[:], R, "wo")
        dy_bf = tile([P, J * PACK], BF16, "dy_bf", "w1_bf")
        interleave(nc.vector.tensor_copy, dy_bf[:, :half * PACK], dy_raw[0][:])
        interleave(nc.scalar.copy, dy_bf[:, half * PACK:], dy_raw[1][:])

        def dealt(ap):
            return ap.rearrange("r (p t) -> r t p", t=PACK)

        def planes(t_):
            return t_[:].rearrange("r (t p) -> r t p", t=PACK)

        a_sum = tile([P, G], F32, "a_sum", "dy_raw0")
        nc.vector.tensor_reduce(a_sum[:], a_ps[:].rearrange("r (g i) -> r g i", i=GROUP), AX.X, ALU.add)
        ce = tile([P, J], F32, "ce")
        for t in range(PACK):
            nc.vector.scalar_tensor_tensor(
                planes(ce)[:, t, :].rearrange("r (g q) -> r g q", q=4), a_sum[:].unsqueeze(2).to_broadcast([P, G, 4]),
                -1.0 / GROUP, dealt(a_ps[:])[:, t, :].rearrange("r (g q) -> r g q", q=4), ALU.mult, ALU.add)
        sq = tile([P, J], F32, "sq", "dy_raw1")
        den2 = tile([P, J], F32, "den2")
        inv_abs = tile([P, J], F32, "inv_abs")
        inv2 = tile([P, J], F32, "inv2")
        halves = [slice(0, half), slice(half, J)]
        for h in halves:
            nc.scalar.activation(sq[:, h], ce[:, h], ACT.Square)
        for h in halves:
            nc.scalar.activation(den2[:, h], sq[:, h], ACT.Square, bias=1.0, scale=s[:])
        for h in halves:
            nc.scalar.activation(inv_abs[:, h], den2[:, h], ACT.Abs_reciprocal_sqrt)
        for h in halves:
            nc.scalar.activation(inv2[:, h], inv_abs[:, h], ACT.Square)
        sca = tile([P, J], F32, "sca")
        nc.vector.scalar_tensor_tensor(planes(sca), planes(ce), s[:], dealt(a_ps[:]), ALU.mult, ALU.mult)

        dy_c, dy_s = quantize(dy_bf[:], J, "dy", "dy_raw0")
        c_ps = ps.tile([P, J], F32, name="c_ps")
        nc.tensor.matmul_mx(out=c_ps[:], lhsT=wo_c[:].bitcast(FP8X4), lhsT_scale=wo_s[:],
                            rhs=dy_c[:].bitcast(FP8X4), rhs_scale=dy_s[:], start=True, stop=True)

        x_g = {}

        def gather_x(t, tag):
            x_g[t] = tile([P, J], BF16, "x_g%d" % t, tag)
            nc.vector.tensor_copy(x_g[t][:], x_win[t][:].indirect(offsets[:]))

        def turn_x(ts, dst):
            name = "".join(str(t) for t in ts)
            xt_ps = ps.tile([P, len(ts), 2, P], F32, name="xt_ps" + name)
            for n, t in enumerate(ts):
                pairs = x_g[t][:].bitcast(F32)
                for u in range(2):
                    nc.tensor.transpose(xt_ps[:, n, u, :], pairs[:, u::2], ident[:])
            nc.scalar.copy(dst.bitcast(F32).rearrange("p (n k u) -> p n k u", k=P, u=2),
                           xt_ps[:].rearrange("p n u k -> p n k u"))

        gather_x(0, "w1_bf")
        x1_bf = tile([P, T], BF16, "x1_bf", "inv_abs")
        nc.scalar.copy(x1_bf[:], x_win[1][:])
        x_g[1] = tile([P, J], BF16, "x_g1")
        nc.scalar.activation(x_g[1][:], x1_bf[:].indirect(offsets[:]), ACT.Copy)

        cv = tile([P, J], F32, "cv", "x_win0")
        dce = tile([P, J], F32, "dce")
        rest = tile([P, J], F32, "rest")
        for n in range(2):
            nc.vector.tensor_tensor(planes(cv)[:, 2 * n:2 * n + 2, :], dealt(c_ps[:])[:, 2 * n:2 * n + 2, :],
                                    planes(inv2)[:, 2 * n:2 * n + 2, :], ALU.mult)
        for h in halves:
            nc.vector.scalar_tensor_tensor(dce[:, h], cv[:, h], -2.0, sca[:, h], ALU.mult, ALU.mult)
        nc.vector.scalar_tensor_tensor(rest[:, halves[0]], sq[:, halves[0]], s[:], cv[:, halves[0]], ALU.mult, ALU.mult)
        d_sum = tile([P, G], F32, "d_sum")
        nc.vector.tensor_reduce(d_sum[:], dce[:].rearrange("r (t g q) -> r g t q", t=PACK, q=4), AX.XY, ALU.add)
        nc.vector.scalar_tensor_tensor(rest[:, halves[1]], sq[:, halves[1]], s[:], cv[:, halves[1]], ALU.mult, ALU.mult)
        back = tile([P, P], F32, "back")
        nc.vector.tensor_scalar(back[:].rearrange("r (g q) -> r g q", q=4),
                                d_sum[:].unsqueeze(2).to_broadcast([P, G, 4]), -1.0 / GROUP, None, ALU.mult)
        da_ps = ps.tile([P, PACK, R], F32, name="da_ps")
        terms = [cv, dce, rest]
        for n, term in enumerate(terms):
            for t in range(PACK):
                nc.tensor.matmul(da_ps[:, t, :], term[:, t * P:(t + 1) * P], ident[:],
                                 start=(n == 0 and t == 0), stop=False, is_transpose=True)
        for t in range(PACK):
            nc.tensor.matmul(da_ps[:, t, :], back[:], ident[:], start=False, stop=(t == PACK - 1), is_transpose=True)

        gather_x(2, "sca")
        x0_gt = tile([P, 2, P * PACK], BF16, "x0_gt", "x_win2")
        turn_x([0], x0_gt[:, 0, :])
        xt_21 = tile([P, 2 * P * PACK], BF16, "xt_21")
        turn_x([2, 1], xt_21[:])
        nc.vector.tensor_tensor(x0_gt[:, 1, :].rearrange("p (r t) -> p r t", t=PACK), da_ps[:].rearrange("p t r -> p r t"),
                                js_col[:].unsqueeze(1).to_broadcast([P, R, PACK]), ALU.mult)
        gather_x(3, None)
        xt_3 = tile([P, P * PACK], BF16, "xt_3")
        turn_x([3], xt_3[:])
        c0g, s0g = quantize(x0_gt[:].rearrange("p n c -> p (n c)"), 2 * P, "x0gt", "x_win3")
        gt_c, gt_s = c0g[:, P:], s0g[:, P:]
        c21, s21 = quantize(xt_21[:], 2 * P, "x21", "x_win2")
        c3, s3 = quantize(xt_3[:], P, "x3")
        xq = {0: (c0g[:, :P], s0g[:, :P]), 1: (c21[:, P:], s21[:, P:]), 2: (c21[:, :P], s21[:, :P]), 3: (c3[:], s3[:])}

        out_v = out.rearrange("(p t) r -> p t r", t=PACK)
        for name, ts in (("early", slice(0, PACK - 1)), ("last", slice(PACK - 1, PACK))):
            count = ts.stop - ts.start
            gw_ps = ps.tile([P, count, R], F32, name="gw_ps_" + name)
            for t in range(ts.start, ts.stop):
                nc.tensor.matmul_mx(out=gw_ps[:, t - ts.start, :], lhsT=xq[t][0].bitcast(FP8X4), lhsT_scale=xq[t][1],
                                    rhs=gt_c.bitcast(FP8X4), rhs_scale=gt_s, start=True, stop=True)
            res = tile([P, count, R], F32, "res_" + name)
            nc.vector.tensor_tensor(res[:], gw_ps[:], old_sb[:, ts, :], ALU.add)
            nc.sync.dma_start(out_v[:, ts, :], res[:])
